import numpy as np
import ml_dtypes


def mxq(x, axis, fmt="e4m3"):
    dtype, down = {"e4m3": (ml_dtypes.float8_e4m3fn, 7), "e5m2": (ml_dtypes.float8_e5m2, 14)}[fmt]
    v = np.moveaxis(np.asarray(x, np.float32).astype(ml_dtypes.bfloat16).astype(np.float64), axis, -1)
    blocks = v.reshape(v.shape[:-1] + (-1, 32))
    amax = np.abs(blocks).max(-1, keepdims=True)
    byte = np.maximum(np.where(amax > 0, np.frexp(amax)[1] - 1 + 127, 0) - down, 1)
    scale = np.exp2(byte - 127.0)
    codes = (blocks / scale).astype(np.float32).astype(dtype).astype(np.float64)
    return np.moveaxis((codes * scale).reshape(v.shape), -1, axis)


WIDE = False


def mx_kscale(k):
    if not WIDE:
        return np.ones(k)
    levels = np.array([10, -10, 5, -5, 0])
    if k % 512:
        return np.exp2(np.random.permutation(np.resize(levels, k // 32))).repeat(32)
    a = np.empty((k // 512, 16))
    for p in range(k // 512):
        a[p, :8] = np.random.permutation(np.resize(levels, 8))
        for g in range(8):
            far = levels[np.abs(levels - a[p, g]) >= 10]
            a[p, g + 8] = far[np.random.randint(len(far))]
    return np.exp2(a.ravel()).repeat(32)


def f64(x):
    return np.asarray(x).astype(np.float64)


def striped(idx):
    return np.tile(idx.reshape(-1, 16).T, (8, 1)).astype(np.uint16)


def unstriped(offs):
    return offs[:16].T.reshape(-1).astype(np.int64)


def striped8(idx):
    return np.concatenate([x.reshape(-1, 16).T for x in idx]).astype(np.uint16)


def runs(offs, k):
    lists = np.stack([offs[16 * r : 16 * r + 16].T.reshape(-1) for r in range(8)]).astype(np.int64)
    return lists[np.arange(k) % 512 // 64]


def pack_weight(w):
    k, n = w.shape
    w = f64(np.asarray(w, np.float32).astype(ml_dtypes.bfloat16)).reshape(k // 32, 32, n)
    amax = np.abs(w).max(1)
    byte = np.clip(np.where(amax > 0, np.frexp(amax)[1] - 1 + 127 - 7, 1), 1, 254)
    scaled = (w * np.exp2(127.0 - byte)[:, None, :]).reshape(k, n).astype(np.float32)
    words = np.ascontiguousarray(scaled.reshape(k // 512, 128, 4, n).transpose(0, 1, 3, 2)).astype(ml_dtypes.float8_e4m3fn).view(np.uint8)
    return words, np.ascontiguousarray(byte.astype(np.uint8).reshape(k // 512, 16, n))


def unpack_weight(words, scales):
    g, p, n, _ = words.shape
    vals = np.ascontiguousarray(words).view(ml_dtypes.float8_e4m3fn).astype(np.float64) * np.repeat(np.exp2(scales.astype(np.float64) - 127.0), 8, axis=1)[..., None]
    return vals.transpose(0, 1, 3, 2).reshape(g * 512, n)


def sigmoid(v):
    return 1.0 / (1.0 + np.exp(-np.maximum(v, -700.0)))


K, T, S, H, C = 512, 2048, 512, 512, 512


def setup_inputs():
    n = np.random.standard_normal
    s = mx_kscale(K)[:, None]
    packed_xT = pack_weight(n((K, T)) * s)
    return {
        "x_words": packed_xT[0],
        "x_scales": packed_xT[1],
        "w1": (n((K, H)) / np.sqrt(K) / s).astype(np.float32),
        "sl": np.random.uniform(1.0, 2.0, (H, 1)).astype(np.float32),
        "th": (0.5 * n((H, 1))).astype(np.float32),
        "gs": (np.random.uniform(0.5, 1.5, (K, 1)) / s).astype(np.float32),
        "sl2": np.random.uniform(1.0, 2.0, (C, 1)).astype(np.float32),
        "th2": (0.5 * n((C, 1))).astype(np.float32),
        "offs": striped(np.random.permutation(T)[:S]),
        "n1": striped8(np.stack([np.random.permutation(S) for _ in range(8)])),
        "ca": striped(np.random.permutation(T)[:C]),
        "hc": striped8(np.random.randint(0, T, (8, C))),
        "n2": striped(np.random.permutation(S)),
        "n3": striped(np.random.permutation(S)),
    }


def reference(x_words, x_scales, w1, sl, th, gs, sl2, th2, offs, n1, ca, hc, n2, n3):
    x_ca = unpack_weight(x_words, x_scales)[:, unstriped(ca)]
    xq = unpack_weight(x_words, x_scales)[:, unstriped(offs)]
    y = mxq(f64(w1), 0, "e4m3").T @ xq
    sg = sigmoid(f64(sl) * (y[np.arange(H)[:, None], runs(n1, H)] - f64(th)))
    z = f64(gs) * (y * sg)
    zq = mxq(z, 0, "e4m3")
    a = 0.0625 * (x_ca.T @ zq)
    x_hc = unpack_weight(x_words, x_scales)[np.arange(K)[:, None], runs(hc, K)]
    b = 0.0625 * (x_hc.T @ zq)
    sg2 = sigmoid(f64(sl2) * (b[:, unstriped(n2)] - f64(th2)))
    return a * sg2 - (0.5 * a[:, unstriped(n3)])

@@ -1,0 +1,305 @@
+from contextlib import ExitStack
+
+import concourse.mybir as mybir
+
+K, T, S, H, C = 512, 2048, 512, 512, 512
+FLOPS = 3 * 2 * 512 * 512 * 512
+
+F32 = mybir.dt.float32
+BF16 = mybir.dt.bfloat16
+I32 = mybir.dt.int32
+U32 = mybir.dt.uint32
+U16 = mybir.dt.uint16
+U8 = mybir.dt.uint8
+FP8X4 = mybir.dt.float8_e4m3fn_x4
+MULT = mybir.AluOpType.mult
+ADD = mybir.AluOpType.add
+COPY = mybir.ActivationFunctionType.Copy
+SIGMOID = mybir.ActivationFunctionType.Sigmoid
+
+P = 128
+PACK = 4
+HALF = 256
+LCOL = HALF // 16
+
+
+def tile_picked_cdhgxbesa_none_p_kernel(
+    tc, x_words, x_scales, w1, sl, th, gs, sl2, th2, offs, n1, ca, hc, n2, n3, out
+):
+    nc = tc.nc
+    with ExitStack() as ctx:
+        lists = ctx.enter_context(tc.tile_pool(name="lists", bufs=1))
+        keep = ctx.enter_context(tc.tile_pool(name="keep", bufs=1))
+        psum = ctx.enter_context(tc.psum_pool(name="psum", bufs=1))
+
+        def list_tile(name):
+            return lists.tile([P, S // 16], U16, name=name)
+
+        offs_t = list_tile("offs_t")
+        n1_t = list_tile("n1_t")
+        ca_t = list_tile("ca_t")
+        hc_t = list_tile("hc_t")
+        n2_t = list_tile("n2_t")
+        n3_t = list_tile("n3_t")
+
+        xw = keep.tile([P, T], U32, name="xw")
+        xs = keep.tile([P, T], U8, name="xs")
+
+        sl_t = keep.tile([P, PACK], F32, name="sl_t")
+        th_t = keep.tile([P, PACK], F32, name="th_t")
+        gs_t = keep.tile([P, PACK], F32, name="gs_t")
+
+        for t_, src in ((sl_t, sl), (th_t, th), (gs_t, gs)):
+            nc.gpsimd.dma_start(out=t_[:], in_=src.rearrange("(p t) o -> p (t o)", t=PACK))
+
+        rows = x_scales[0].bitcast(I32)
+        nc.sync.dma_start(
+            out=xs[:].bitcast(I32), in_=rows.unsqueeze(1).to_broadcast([16, 8, T // 4])
+        )
+        nc.sync.dma_start(offs_t[:], offs)
+        nc.sync.dma_start(hc_t[:], hc)
+        nc.sync.dma_start(ca_t[:], ca)
+        nc.sync.dma_start(n1_t[:], n1)
+        nc.sync.dma_start(
+            out=xw[:].bitcast(I32),
+            in_=x_words[0].rearrange("p n t -> p (n t)").bitcast(I32),
+        )
+        w_rows = w1.rearrange("(p j) c -> p j c", j=PACK)
+        w_raw = []
+        for h in range(2):
+            wr = keep.tile([P, PACK, HALF], F32, name="w_raw%d" % h, tag="w_raw%d" % h)
+            nc.sync.dma_start(out=wr[:], in_=w_rows[:, :, h * HALF : (h + 1) * HALF])
+            w_raw.append(wr)
+        nc.sync.dma_start(n2_t[:], n2)
+        nc.sync.dma_start(n3_t[:], n3)
+
+        def place(queue, placed, picked):
+            for a in range(4):
+                queue.dma_start(
+                    out=placed[a:P:32, :].bitcast(I32),
+                    in_=picked[8 * a : P : 32, :].bitcast(I32),
+                )
+
+        xq_s = keep.tile([P, S], U8, name="xq_s", align_bytes=64)
+        nc.vector.memset(xq_s[:].bitcast(I32), 0)
+        cand_s = keep.tile([P, 2 * C], U8, name="cand_s", align_bytes=64)
+        nc.vector.memset(cand_s[:].bitcast(I32), 0)
+        xq_g = keep.tile([P, S], U8, name="xq_g")
+        nc.vector.tensor_copy(xq_g[:], xs[:].indirect(offs_t[:]))
+        place(nc.scalar, xq_s, xq_g)
+        cand_g = keep.tile([P, 2 * C], U8, name="cand_g")
+        nc.vector.tensor_copy(cand_g[:, 0:C], xs[:].indirect(hc_t[:]))
+        xq_w = keep.tile([P, S], U32, name="xq_w", align_bytes=64)
+        nc.vector.tensor_copy(xq_w[:], xw[:].indirect(offs_t[:]))
+        nc.vector.tensor_copy(cand_g[:, C : 2 * C], xs[:].indirect(ca_t[:]))
+        place(nc.sync, cand_s, cand_g)
+        hc_s = cand_s[:, 0:C]
+        ca_s = cand_s[:, C : 2 * C]
+        hc_w = keep.tile([P, C], U32, name="hc_w", align_bytes=64)
+        nc.vector.tensor_copy(hc_w[:], xw[:].indirect(hc_t[:]))
+
+        wg = keep.tile([P, PACK * P * PACK], BF16, name="wg", align_bytes=64, tag="wg")
+        wg_v = wg[:].rearrange("p (t m j) -> p m j t", t=PACK, j=PACK)
+        for h in range(2):
+            src = w_raw[h][:].rearrange("p j (m t) -> p m j t", t=PACK)
+            nc.scalar.copy(out=wg_v[:, 64 * h : 64 * (h + 1)], in_=src)
+        sl2_t = keep.tile([P, PACK], F32, name="sl2_t", tag="w_raw0")
+        th2_t = keep.tile([P, PACK], F32, name="th2_t", tag="w_raw1")
+        with nc.allow_non_contiguous_dma(reason="one value a row"):
+            for t_, src in ((sl2_t, sl2), (th2_t, th2)):
+                nc.sync.dma_start(out=t_[:], in_=src.rearrange("(c p) o -> p (c o)", p=P))
+        wq_w = keep.tile([P, H], U32, name="wq_w", align_bytes=64)
+        wq_s = keep.tile([P, H], U8, name="wq_s", align_bytes=64)
+        for t in range(PACK):
+            nc.vector.quantize_mx(
+                out=wq_w[:, t * P : (t + 1) * P].bitcast(FP8X4),
+                scales=wq_s[:, t * P : (t + 1) * P],
+                in_=wg[:, t * 512 : (t + 1) * 512],
+            )
+
+        nb1 = keep.tile([P, PACK], F32, name="nb1")
+        nc.vector.scalar_tensor_tensor(nb1[:], sl_t[:], -1.0, th_t[:], MULT, MULT)
+
+        y_ps = []
+        for t in range(PACK):
+            bank = psum.tile([P, S], F32, name="y_ps%d" % t, tag="bank%d" % t)
+            nc.tensor.matmul_mx(
+                out=bank[:],
+                lhsT=wq_w[:, t * P : (t + 1) * P].bitcast(FP8X4),
+                lhsT_scale=wq_s[:, t * P : (t + 1) * P],
+                rhs=xq_w[:].bitcast(FP8X4),
+                rhs_scale=xq_s[:],
+                start=True,
+                stop=True,
+            )
+            y_ps.append(bank)
+        y_sb = [keep.tile([P, S], F32, name="y_sb%d" % t) for t in range(PACK)]
+
+        ca_w = keep.tile([P, C], U32, name="ca_w", align_bytes=64, tag="wg")
+        nc.vector.tensor_copy(ca_w[:], xw[:].indirect(ca_t[:]))
+
+        ab_sb = [[keep.tile([P, S], F32, name="ab_sb%d%d" % (kind, c)) for c in range(PACK)] for kind in range(2)]
+        cand = ((hc_w, hc_s), (ca_w, ca_s))
+        ab_ps = {}
+
+        def open_banks():
+            for c in range(PACK):
+                for kind in range(2):
+                    n = (2 * c + kind + 4) % 8
+                    ab_ps[(kind, c)] = psum.tile([P, S], F32, name="ab_ps%d%d" % (kind, c), tag="bank%d" % n)
+
+        def product(kind, c, lo, hi, zq_w, zq_s):
+            words, scales = cand[kind]
+            nc.tensor.matmul_mx(
+                out=ab_ps[(kind, c)][:, lo:hi],
+                lhsT=words[:, c * P : (c + 1) * P].bitcast(FP8X4),
+                lhsT_scale=scales[:, c * P : (c + 1) * P],
+                rhs=zq_w[:].bitcast(FP8X4),
+                rhs_scale=zq_s[:],
+                start=True,
+                stop=True,
+            )
+
+        parts = ((0, 384), (384, 512))
+
+        def leave(g, kind, c, on_vector):
+            lo, hi = parts[g]
+            dst = ab_sb[kind][c][:, lo:hi]
+            src = ab_ps[(kind, c)][:, lo:hi]
+            factor = (0.0625, -0.03125)[kind]
+            if on_vector:
+                nc.vector.tensor_scalar(dst, src, factor, None, MULT)
+            else:
+                nc.scalar.activation(dst, src, COPY, scale=factor)
+
+        pieces = ((0, 128), (128, 384), (384, 512))
+        sg = {}
+        zp = {}
+        zi = {}
+        zq = {}
+
+        def gate(i, t):
+            lo, hi = pieces[i]
+            if t == 0:
+                sg[i] = keep.tile([P, PACK, hi - lo], F32, name="sg%d" % i)
+                zp[i] = keep.tile([P, PACK, hi - lo], BF16, name="zp%d" % i)
+            nc.scalar.activation(
+                sg[i][:, t, :],
+                y_sb[t][:].indirect(n1_t[:, lo // 16 : hi // 16]),
+                SIGMOID,
+                bias=nb1[:, t : t + 1],
+                scale=sl_t[:, t : t + 1],
+            )
+
+        def weigh(i, t):
+            lo, hi = pieces[i]
+            nc.vector.scalar_tensor_tensor(
+                zp[i][:, t, :], y_sb[t][:, lo:hi], gs_t[:, t : t + 1], sg[i][:, t, :], MULT, MULT
+            )
+
+        def weave(i):
+            lo, hi = pieces[i]
+            zi[i] = keep.tile([P, (hi - lo) * PACK], BF16, name="zi%d" % i, align_bytes=64)
+            nc.vector.tensor_copy(
+                zi[i][:].rearrange("p (c i t) -> p c t i", i=4, t=PACK),
+                zp[i][:].rearrange("p t (c i) -> p c t i", i=4),
+            )
+
+        def quantise(i):
+            lo, hi = pieces[i]
+            zq_w = keep.tile([P, hi - lo], U32, name="zq_w%d" % i, align_bytes=64)
+            zq_s = keep.tile([P, hi - lo], U8, name="zq_s%d" % i, align_bytes=64)
+            nc.vector.quantize_mx(out=zq_w[:].bitcast(FP8X4), scales=zq_s[:], in_=zi[i][:])
+            zq[i] = (zq_w, zq_s)
+
+        def products(i, tiles):
+            lo, hi = pieces[i]
+            for c in tiles:
+                for kind in range(2):
+                    product(kind, c, lo, hi, zq[i][0], zq[i][1])
+
+        nc.scalar.copy(y_sb[0][:], y_ps[0][:])
+        nc.vector.tensor_copy(y_sb[1][:], y_ps[1][:])
+        gate(0, 0)
+        nc.scalar.copy(y_sb[2][:], y_ps[2][:])
+        nc.vector.tensor_copy(y_sb[3][:], y_ps[3][:])
+        for t in range(1, PACK):
+            gate(0, t)
+        for t in range(PACK):
+            weigh(0, t)
+        for i in (1, 2):
+            for t in range(PACK):
+                gate(i, t)
+        weave(0)
+        nb2 = keep.tile([P, PACK], F32, name="nb2")
+        nc.vector.scalar_tensor_tensor(nb2[:], sl2_t[:], -1.0, th2_t[:], MULT, MULT)
+        weigh(1, 0)
+        quantise(0)
+        open_banks()
+        products(0, range(PACK))
+        for t in range(1, PACK):
+            weigh(1, t)
+        weigh(2, 0)
+        weave(1)
+        weigh(2, 1)
+        quantise(1)
+        products(1, range(PACK))
+        weigh(2, 2)
+        weigh(2, 3)
+        weave(2)
+        quantise(2)
+        for c in (0, 1):
+            for kind in range(2):
+                leave(0, kind, c, False)
+        products(2, (0, 1))
+        for c in (2, 3):
+            leave(0, 1, c, True)
+        leave(1, 0, 0, False)
+        leave(1, 1, 0, True)
+
+        a_sb = ab_sb[1]
+        b_sb = ab_sb[0]
+        res = [keep.tile([P, S], F32, name="res%d" % c) for c in range(PACK)]
+        prod = {}
+
+        def score(c, q):
+            cols = slice(q * HALF, (q + 1) * HALF)
+            sg2 = keep.tile([P, HALF], F32, name="sg2_%d" % (2 * c + q))
+            nc.scalar.activation(
+                sg2[:],
+                b_sb[c][:].indirect(n2_t[:, q * LCOL : (q + 1) * LCOL]),
+                SIGMOID,
+                bias=nb2[:, c : c + 1],
+                scale=sl2_t[:, c : c + 1],
+            )
+            prod[(c, q)] = keep.tile([P, HALF], F32, name="prod%d" % (2 * c + q))
+            nc.vector.scalar_tensor_tensor(prod[(c, q)][:], a_sb[c][:, cols], -2.0, sg2[:], MULT, MULT)
+
+        def finish(c, q):
+            cols = slice(q * HALF, (q + 1) * HALF)
+            picked = a_sb[c][:].indirect(n3_t[:, q * LCOL : (q + 1) * LCOL])
+            if c < PACK - 1:
+                nc.vector.tensor_tensor(res[c][:, cols], picked, prod[(c, q)][:], ADD)
+                if q == 1:
+                    nc.sync.dma_start(out=out[c * P : (c + 1) * P, :], in_=res[c][:])
+            else:
+                far = keep.tile([P, HALF], F32, name="far%d" % q)
+                nc.scalar.activation(far[:], picked, COPY)
+                nc.vector.tensor_tensor(res[c][:, cols], far[:], prod[(c, q)][:], ADD)
+                nc.sync.dma_start(out=out[c * P : (c + 1) * P, cols], in_=res[c][:, cols])
+
+        steps = [(c, q) for c in range(PACK) for q in range(2)]
+        for k, (c, q) in enumerate(steps):
+            if k == 2:
+                leave(1, 0, 1, False)
+                leave(1, 1, 1, False)
+            if q == 0 and c >= 2:
+                leave(0, 0, c, False)
+                products(2, (c,))
+                leave(1, 1, c, False)
+                leave(1, 0, c, False)
+            score(c, q)
+            if 1 <= k < 7:
+                finish(*steps[k - 1])
+        finish(3, 0)
+        finish(3, 1)

@@ -21,6 +21,7 @@ P = 128
 PACK = 4
 HALF = 256
 LCOL = HALF // 16
+SHARE = 24
 
 
 def tile_picked_cdhgxbesa_none_p_kernel(
@@ -49,8 +50,18 @@ def tile_picked_cdhgxbesa_none_p_kernel(
         th_t = keep.tile([P, PACK], F32, name="th_t")
         gs_t = keep.tile([P, PACK], F32, name="gs_t")
 
+        row_sb = [keep.tile([P, 2 * S], F32, name="row_sb%d" % t) for t in range(PACK)]
+        a_sb = [keep.tile([P, S + 8], F32, name="a_sb%d" % c) for c in range(PACK)]
         for t_, src in ((sl_t, sl), (th_t, th), (gs_t, gs)):
             nc.gpsimd.dma_start(out=t_[:], in_=src.rearrange("(p t) o -> p (t o)", t=PACK))
+        for t in range(PACK):
+            nc.gpsimd.memset(row_sb[t][:, S : 2 * S], 0.0)
+        for t in range(PACK):
+            nc.gpsimd.memset(a_sb[t][:, S : S + 8], 0.0)
+        warm = keep.tile([P, 1], F32, name="warm")
+        nc.vector.memset(warm[:], 0.0)
+        warm2 = keep.tile([P, 1], F32, name="warm2")
+        nc.scalar.activation(warm2[:], warm[:], SIGMOID)
 
         rows = x_scales[0].bitcast(I32)
         nc.sync.dma_start(
@@ -59,7 +70,6 @@ def tile_picked_cdhgxbesa_none_p_kernel(
         nc.sync.dma_start(offs_t[:], offs)
         nc.sync.dma_start(hc_t[:], hc)
         nc.sync.dma_start(ca_t[:], ca)
-        nc.sync.dma_start(n1_t[:], n1)
         nc.sync.dma_start(
             out=xw[:].bitcast(I32),
             in_=x_words[0].rearrange("p n t -> p (n t)").bitcast(I32),
@@ -70,31 +80,30 @@ def tile_picked_cdhgxbesa_none_p_kernel(
             wr = keep.tile([P, PACK, HALF], F32, name="w_raw%d" % h, tag="w_raw%d" % h)
             nc.sync.dma_start(out=wr[:], in_=w_rows[:, :, h * HALF : (h + 1) * HALF])
             w_raw.append(wr)
+        nc.sync.dma_start(n1_t[:], n1)
         nc.sync.dma_start(n2_t[:], n2)
         nc.sync.dma_start(n3_t[:], n3)
 
-        def place(queue, placed, picked):
-            for a in range(4):
-                queue.dma_start(
-                    out=placed[a:P:32, :].bitcast(I32),
-                    in_=picked[8 * a : P : 32, :].bitcast(I32),
-                )
+        def negated_product(dst, slope, threshold, name):
+            both = keep.tile([P, PACK], F32, name=name)
+            nc.gpsimd.tensor_tensor(both[:], slope[:], threshold[:], MULT)
+            nc.gpsimd.tensor_scalar(dst[:], both[:], -1.0, 0.0, MULT, ADD)
 
-        xq_s = keep.tile([P, S], U8, name="xq_s", align_bytes=64)
-        nc.vector.memset(xq_s[:].bitcast(I32), 0)
-        cand_s = keep.tile([P, 2 * C], U8, name="cand_s", align_bytes=64)
-        nc.vector.memset(cand_s[:].bitcast(I32), 0)
-        xq_g = keep.tile([P, S], U8, name="xq_g")
-        nc.vector.tensor_copy(xq_g[:], xs[:].indirect(offs_t[:]))
-        place(nc.scalar, xq_s, xq_g)
-        cand_g = keep.tile([P, 2 * C], U8, name="cand_g")
-        nc.vector.tensor_copy(cand_g[:, 0:C], xs[:].indirect(hc_t[:]))
+        picked_s = keep.tile([P, 3 * S], U8, name="picked_s")
+        for n, lst in enumerate((offs_t, hc_t, ca_t)):
+            nc.vector.tensor_copy(picked_s[:, n * S : (n + 1) * S], xs[:].indirect(lst[:]))
+        placed_s = keep.tile([P, 3 * S], U8, name="placed_s", align_bytes=64)
+        nc.vector.tensor_copy(placed_s[:].bitcast(I32), picked_s[:].bitcast(I32))
+        for a in range(1, 4):
+            nc.scalar.dma_start(
+                out=placed_s[a:P:32, :].bitcast(I32),
+                in_=picked_s[8 * a : P : 32, :].bitcast(I32),
+            )
+        xq_s = placed_s[:, 0:S]
+        hc_s = placed_s[:, S : 2 * S]
+        ca_s = placed_s[:, 2 * S : 3 * S]
         xq_w = keep.tile([P, S], U32, name="xq_w", align_bytes=64)
         nc.vector.tensor_copy(xq_w[:], xw[:].indirect(offs_t[:]))
-        nc.vector.tensor_copy(cand_g[:, C : 2 * C], xs[:].indirect(ca_t[:]))
-        place(nc.sync, cand_s, cand_g)
-        hc_s = cand_s[:, 0:C]
-        ca_s = cand_s[:, C : 2 * C]
         hc_w = keep.tile([P, C], U32, name="hc_w", align_bytes=64)
         nc.vector.tensor_copy(hc_w[:], xw[:].indirect(hc_t[:]))
 
@@ -102,7 +111,11 @@ def tile_picked_cdhgxbesa_none_p_kernel(
         wg_v = wg[:].rearrange("p (t m j) -> p m j t", t=PACK, j=PACK)
         for h in range(2):
             src = w_raw[h][:].rearrange("p j (m t) -> p m j t", t=PACK)
-            nc.scalar.copy(out=wg_v[:, 64 * h : 64 * (h + 1)], in_=src)
+            if h == 0:
+                nc.scalar.copy(out=wg_v[:, 0:64], in_=src)
+            else:
+                nc.scalar.copy(out=wg_v[:, 64 : 64 + SHARE], in_=src[:, 0:SHARE])
+                nc.vector.tensor_copy(out=wg_v[:, 64 + SHARE : 128], in_=src[:, SHARE:64])
         sl2_t = keep.tile([P, PACK], F32, name="sl2_t", tag="w_raw0")
         th2_t = keep.tile([P, PACK], F32, name="th2_t", tag="w_raw1")
         with nc.allow_non_contiguous_dma(reason="one value a row"):
@@ -118,7 +131,7 @@ def tile_picked_cdhgxbesa_none_p_kernel(
             )
 
         nb1 = keep.tile([P, PACK], F32, name="nb1")
-        nc.vector.scalar_tensor_tensor(nb1[:], sl_t[:], -1.0, th_t[:], MULT, MULT)
+        negated_product(nb1, sl_t, th_t, "slth")
 
         y_ps = []
         for t in range(PACK):
@@ -128,178 +141,131 @@ def tile_picked_cdhgxbesa_none_p_kernel(
                 lhsT=wq_w[:, t * P : (t + 1) * P].bitcast(FP8X4),
                 lhsT_scale=wq_s[:, t * P : (t + 1) * P],
                 rhs=xq_w[:].bitcast(FP8X4),
-                rhs_scale=xq_s[:],
+                rhs_scale=xq_s,
                 start=True,
                 stop=True,
             )
             y_ps.append(bank)
-        y_sb = [keep.tile([P, S], F32, name="y_sb%d" % t) for t in range(PACK)]
 
         ca_w = keep.tile([P, C], U32, name="ca_w", align_bytes=64, tag="wg")
         nc.vector.tensor_copy(ca_w[:], xw[:].indirect(ca_t[:]))
 
-        ab_sb = [[keep.tile([P, S], F32, name="ab_sb%d%d" % (kind, c)) for c in range(PACK)] for kind in range(2)]
-        cand = ((hc_w, hc_s), (ca_w, ca_s))
-        ab_ps = {}
+        whole = slice(0, S)
+        halves = (slice(0, HALF), slice(HALF, S))
 
-        def open_banks():
-            for c in range(PACK):
-                for kind in range(2):
-                    n = (2 * c + kind + 4) % 8
-                    ab_ps[(kind, c)] = psum.tile([P, S], F32, name="ab_ps%d%d" % (kind, c), tag="bank%d" % n)
+        def offsets(lst, cols):
+            return lst[:, cols.start // 16 : cols.stop // 16]
 
-        def product(kind, c, lo, hi, zq_w, zq_s):
-            words, scales = cand[kind]
-            nc.tensor.matmul_mx(
-                out=ab_ps[(kind, c)][:, lo:hi],
-                lhsT=words[:, c * P : (c + 1) * P].bitcast(FP8X4),
-                lhsT_scale=scales[:, c * P : (c + 1) * P],
-                rhs=zq_w[:].bitcast(FP8X4),
-                rhs_scale=zq_s[:],
-                start=True,
-                stop=True,
-            )
+        nc.scalar.copy(row_sb[0][:, 0:S], y_ps[0][:])
+        for t in range(1, PACK):
+            nc.vector.tensor_copy(row_sb[t][:, 0:S], y_ps[t][:])
 
-        parts = ((0, 384), (384, 512))
+        zp = keep.tile([P, PACK, S], BF16, name="zp")
+        zq_w = keep.tile([P, S], U32, name="zq_w", align_bytes=64)
+        zq_s = keep.tile([P, S], U8, name="zq_s", align_bytes=64)
 
-        def leave(g, kind, c, on_vector):
-            lo, hi = parts[g]
-            dst = ab_sb[kind][c][:, lo:hi]
-            src = ab_ps[(kind, c)][:, lo:hi]
-            factor = (0.0625, -0.03125)[kind]
-            if on_vector:
-                nc.vector.tensor_scalar(dst, src, factor, None, MULT)
-            else:
-                nc.scalar.activation(dst, src, COPY, scale=factor)
-
-        pieces = ((0, 128), (128, 384), (384, 512))
-        sg = {}
-        zp = {}
-        zi = {}
-        zq = {}
-
-        def gate(i, t):
-            lo, hi = pieces[i]
-            if t == 0:
-                sg[i] = keep.tile([P, PACK, hi - lo], F32, name="sg%d" % i)
-                zp[i] = keep.tile([P, PACK, hi - lo], BF16, name="zp%d" % i)
+        def gate(t, cols):
+            sg = keep.tile([P, cols.stop - cols.start], F32, name="sg%d_%d" % (t, cols.start), tag="sg%d" % t)
             nc.scalar.activation(
-                sg[i][:, t, :],
-                y_sb[t][:].indirect(n1_t[:, lo // 16 : hi // 16]),
+                sg[:],
+                row_sb[t][:].indirect(offsets(n1_t, cols)),
                 SIGMOID,
                 bias=nb1[:, t : t + 1],
                 scale=sl_t[:, t : t + 1],
             )
-
-        def weigh(i, t):
-            lo, hi = pieces[i]
             nc.vector.scalar_tensor_tensor(
-                zp[i][:, t, :], y_sb[t][:, lo:hi], gs_t[:, t : t + 1], sg[i][:, t, :], MULT, MULT
+                zp[:, t, cols], row_sb[t][:, cols], gs_t[:, t : t + 1], sg[:], MULT, MULT
             )
 
-        def weave(i):
-            lo, hi = pieces[i]
-            zi[i] = keep.tile([P, (hi - lo) * PACK], BF16, name="zi%d" % i, align_bytes=64)
-            nc.vector.tensor_copy(
-                zi[i][:].rearrange("p (c i t) -> p c t i", i=4, t=PACK),
-                zp[i][:].rearrange("p t (c i) -> p c t i", i=4),
+        def weave(h):
+            zi = keep.tile([P, HALF * PACK], BF16, name="zi%d" % h, tag="zi%d" % h, align_bytes=64)
+            woven = zi[:].rearrange("p (c i t) -> p c t i", i=4, t=PACK)
+            planes = zp[:, :, halves[h]].rearrange("p t (c i) -> p c t i", i=4)
+            nc.vector.tensor_copy(woven, planes)
+            return zi
+
+        def quantise(h, zi):
+            nc.vector.quantize_mx(out=zq_w[:, halves[h]].bitcast(FP8X4), scales=zq_s[:, halves[h]], in_=zi[:])
+
+        def product(bank, words, scales, cols):
+            nc.tensor.matmul_mx(
+                out=bank[:, cols],
+                lhsT=words.bitcast(FP8X4),
+                lhsT_scale=scales,
+                rhs=zq_w[:, cols].bitcast(FP8X4),
+                rhs_scale=zq_s[:, cols],
+                start=True,
+                stop=True,
             )
 
-        def quantise(i):
-            lo, hi = pieces[i]
-            zq_w = keep.tile([P, hi - lo], U32, name="zq_w%d" % i, align_bytes=64)
-            zq_s = keep.tile([P, hi - lo], U8, name="zq_s%d" % i, align_bytes=64)
-            nc.vector.quantize_mx(out=zq_w[:].bitcast(FP8X4), scales=zq_s[:], in_=zi[i][:])
-            zq[i] = (zq_w, zq_s)
+        b_ps = {}
+        a_ps = {}
 
-        def products(i, tiles):
-            lo, hi = pieces[i]
-            for c in tiles:
-                for kind in range(2):
-                    product(kind, c, lo, hi, zq[i][0], zq[i][1])
+        def product_b(c, cols):
+            if c not in b_ps:
+                b_ps[c] = psum.tile([P, S], F32, name="b_ps%d" % c, tag="bank%d" % (4 + c))
+            product(b_ps[c], hc_w[:, c * P : (c + 1) * P], hc_s[:, c * P : (c + 1) * P], cols)
 
-        nc.scalar.copy(y_sb[0][:], y_ps[0][:])
-        nc.vector.tensor_copy(y_sb[1][:], y_ps[1][:])
-        gate(0, 0)
-        nc.scalar.copy(y_sb[2][:], y_ps[2][:])
-        nc.vector.tensor_copy(y_sb[3][:], y_ps[3][:])
-        for t in range(1, PACK):
-            gate(0, t)
-        for t in range(PACK):
-            weigh(0, t)
-        for i in (1, 2):
-            for t in range(PACK):
-                gate(i, t)
-        weave(0)
-        nb2 = keep.tile([P, PACK], F32, name="nb2")
-        nc.vector.scalar_tensor_tensor(nb2[:], sl2_t[:], -1.0, th2_t[:], MULT, MULT)
-        weigh(1, 0)
-        quantise(0)
-        open_banks()
-        products(0, range(PACK))
-        for t in range(1, PACK):
-            weigh(1, t)
-        weigh(2, 0)
-        weave(1)
-        weigh(2, 1)
-        quantise(1)
-        products(1, range(PACK))
-        weigh(2, 2)
-        weigh(2, 3)
-        weave(2)
-        quantise(2)
-        for c in (0, 1):
-            for kind in range(2):
-                leave(0, kind, c, False)
-        products(2, (0, 1))
-        for c in (2, 3):
-            leave(0, 1, c, True)
-        leave(1, 0, 0, False)
-        leave(1, 1, 0, True)
+        def product_a(c, cols):
+            if c not in a_ps:
+                a_ps[c] = psum.tile([P, S], F32, name="a_ps%d" % c, tag="bank%d" % c)
+            product(a_ps[c], ca_w[:, c * P : (c + 1) * P], ca_s[:, c * P : (c + 1) * P], cols)
 
-        a_sb = ab_sb[1]
-        b_sb = ab_sb[0]
-        res = [keep.tile([P, S], F32, name="res%d" % c) for c in range(PACK)]
-        prod = {}
+        def leave_b(c, cols):
+            nc.scalar.activation(row_sb[c][:, cols], b_ps[c][:, cols], COPY, scale=0.0625)
 
-        def score(c, q):
-            cols = slice(q * HALF, (q + 1) * HALF)
-            sg2 = keep.tile([P, HALF], F32, name="sg2_%d" % (2 * c + q))
-            nc.scalar.activation(
-                sg2[:],
-                b_sb[c][:].indirect(n2_t[:, q * LCOL : (q + 1) * LCOL]),
-                SIGMOID,
-                bias=nb2[:, c : c + 1],
-                scale=sl2_t[:, c : c + 1],
-            )
-            prod[(c, q)] = keep.tile([P, HALF], F32, name="prod%d" % (2 * c + q))
-            nc.vector.scalar_tensor_tensor(prod[(c, q)][:], a_sb[c][:, cols], -2.0, sg2[:], MULT, MULT)
-
-        def finish(c, q):
-            cols = slice(q * HALF, (q + 1) * HALF)
-            picked = a_sb[c][:].indirect(n3_t[:, q * LCOL : (q + 1) * LCOL])
-            if c < PACK - 1:
-                nc.vector.tensor_tensor(res[c][:, cols], picked, prod[(c, q)][:], ADD)
-                if q == 1:
-                    nc.sync.dma_start(out=out[c * P : (c + 1) * P, :], in_=res[c][:])
+        def leave_a(c, cols, on_vector):
+            if on_vector:
+                nc.vector.tensor_scalar(a_sb[c][:, cols], a_ps[c][:, cols], -0.03125, None, MULT)
             else:
-                far = keep.tile([P, HALF], F32, name="far%d" % q)
-                nc.scalar.activation(far[:], picked, COPY)
-                nc.vector.tensor_tensor(res[c][:, cols], far[:], prod[(c, q)][:], ADD)
-                nc.sync.dma_start(out=out[c * P : (c + 1) * P, cols], in_=res[c][:, cols])
+                nc.scalar.activation(a_sb[c][:, cols], a_ps[c][:, cols], COPY, scale=-0.03125)
 
-        steps = [(c, q) for c in range(PACK) for q in range(2)]
-        for k, (c, q) in enumerate(steps):
-            if k == 2:
-                leave(1, 0, 1, False)
-                leave(1, 1, 1, False)
-            if q == 0 and c >= 2:
-                leave(0, 0, c, False)
-                products(2, (c,))
-                leave(1, 1, c, False)
-                leave(1, 0, c, False)
-            score(c, q)
-            if 1 <= k < 7:
-                finish(*steps[k - 1])
-        finish(3, 0)
-        finish(3, 1)
+        gate(0, whole)
+        for t in range(1, PACK):
+            gate(t, halves[0])
+        gate(1, halves[1])
+        quantise(0, weave(0))
+        gate(2, halves[1])
+        gate(3, halves[1])
+        for c in range(PACK):
+            product_b(c, halves[0])
+            product_a(c, halves[0])
+        quantise(1, weave(1))
+        nb2 = keep.tile([P, PACK], F32, name="nb2")
+        negated_product(nb2, sl2_t, th2_t, "slth2")
+        for c in range(PACK):
+            leave_b(c, halves[0])
+            leave_a(c, halves[0], False)
+        for c in range(PACK):
+            product_b(c, halves[1])
+            product_a(c, halves[1])
+        for c in range(PACK):
+            leave_a(c, halves[1], True)
+
+        prod = keep.tile([P, PACK, S], F32, name="prod")
+        res = keep.tile([P, PACK, S], F32, name="res")
+        last = PACK - 1
+        for c in range(PACK):
+            leave_b(c, halves[1])
+            sg2 = keep.tile([P, S], F32, name="sg2_%d" % c, tag="sg2_%d" % c)
+            for cols in halves if c in (0, last) else (whole,):
+                nc.scalar.activation(
+                    sg2[:, cols],
+                    row_sb[c][:].indirect(offsets(n2_t, cols)),
+                    SIGMOID,
+                    bias=nb2[:, c : c + 1],
+                    scale=sl2_t[:, c : c + 1],
+                )
+            for cols in halves:
+                nc.vector.scalar_tensor_tensor(prod[:, c, cols], a_sb[c][:, cols], -2.0, sg2[:, cols], MULT, MULT)
+            for h, cols in enumerate(halves):
+                picked = a_sb[c][:].indirect(offsets(n3_t, cols))
+                if c < last:
+                    nc.vector.tensor_tensor(res[:, c, cols], picked, prod[:, c, cols], ADD)
+                else:
+                    far = keep.tile([P, HALF], F32, name="far%d" % h, tag="sg2_%d" % (1 + h))
+                    nc.scalar.activation(far[:], picked, COPY)
+                    nc.vector.tensor_tensor(res[:, c, cols], far[:], prod[:, c, cols], ADD)
+                    nc.sync.dma_start(out=out[c * P : (c + 1) * P, cols], in_=res[:, c, cols])
+            if c < last:
+                nc.sync.dma_start(out=out[c * P : (c + 1) * P, :], in_=res[:, c, :])

@@ -21,7 +21,7 @@ P = 128
 PACK = 4
 HALF = 256
 LCOL = HALF // 16
-SHARE = 24
+SHARE = 44
 
 
 def tile_picked_cdhgxbesa_none_p_kernel(
@@ -89,13 +89,13 @@ def tile_picked_cdhgxbesa_none_p_kernel(
             nc.gpsimd.tensor_tensor(both[:], slope[:], threshold[:], MULT)
             nc.gpsimd.tensor_scalar(dst[:], both[:], -1.0, 0.0, MULT, ADD)
 
+        placed_s = keep.tile([P, 3 * S], U8, name="placed_s", align_bytes=64)
+        nc.vector.memset(placed_s[:].bitcast(I32), 0)
         picked_s = keep.tile([P, 3 * S], U8, name="picked_s")
         for n, lst in enumerate((offs_t, hc_t, ca_t)):
             nc.vector.tensor_copy(picked_s[:, n * S : (n + 1) * S], xs[:].indirect(lst[:]))
-        placed_s = keep.tile([P, 3 * S], U8, name="placed_s", align_bytes=64)
-        nc.vector.tensor_copy(placed_s[:].bitcast(I32), picked_s[:].bitcast(I32))
-        for a in range(1, 4):
-            nc.scalar.dma_start(
+        for a in range(4):
+            nc.sync.dma_start(
                 out=placed_s[a:P:32, :].bitcast(I32),
                 in_=picked_s[8 * a : P : 32, :].bitcast(I32),
             )

from contextlib import ExitStack

import concourse.mybir as mybir

K, T, S, H, C = 512, 2048, 512, 512, 512
FLOPS = 3 * 2 * 512 * 512 * 512

F32 = mybir.dt.float32
BF16 = mybir.dt.bfloat16
I32 = mybir.dt.int32
U32 = mybir.dt.uint32
U16 = mybir.dt.uint16
U8 = mybir.dt.uint8
FP8X4 = mybir.dt.float8_e4m3fn_x4
MULT = mybir.AluOpType.mult
ADD = mybir.AluOpType.add
COPY = mybir.ActivationFunctionType.Copy
SIGMOID = mybir.ActivationFunctionType.Sigmoid

P = 128
PACK = 4
HALF = 256
LCOL = HALF // 16
SHARE = 44


def tile_picked_cdhgxbesa_none_p_kernel(
    tc, x_words, x_scales, w1, sl, th, gs, sl2, th2, offs, n1, ca, hc, n2, n3, out
):
    nc = tc.nc
    with ExitStack() as ctx:
        lists = ctx.enter_context(tc.tile_pool(name="lists", bufs=1))
        keep = ctx.enter_context(tc.tile_pool(name="keep", bufs=1))
        psum = ctx.enter_context(tc.psum_pool(name="psum", bufs=1))

        def list_tile(name):
            return lists.tile([P, S // 16], U16, name=name)

        offs_t = list_tile("offs_t")
        n1_t = list_tile("n1_t")
        ca_t = list_tile("ca_t")
        hc_t = list_tile("hc_t")
        n2_t = list_tile("n2_t")
        n3_t = list_tile("n3_t")

        xw = keep.tile([P, T], U32, name="xw")
        xs = keep.tile([P, T], U8, name="xs")

        sl_t = keep.tile([P, PACK], F32, name="sl_t")
        th_t = keep.tile([P, PACK], F32, name="th_t")
        gs_t = keep.tile([P, PACK], F32, name="gs_t")

        row_sb = [keep.tile([P, 2 * S], F32, name="row_sb%d" % t) for t in range(PACK)]
        a_sb = [keep.tile([P, S + 8], F32, name="a_sb%d" % c) for c in range(PACK)]
        for t_, src in ((sl_t, sl), (th_t, th), (gs_t, gs)):
            nc.gpsimd.dma_start(out=t_[:], in_=src.rearrange("(p t) o -> p (t o)", t=PACK))
        for t in range(PACK):
            nc.gpsimd.memset(row_sb[t][:, S : 2 * S], 0.0)
        for t in range(PACK):
            nc.gpsimd.memset(a_sb[t][:, S : S + 8], 0.0)
        warm = keep.tile([P, 1], F32, name="warm")
        nc.vector.memset(warm[:], 0.0)
        warm2 = keep.tile([P, 1], F32, name="warm2")
        nc.scalar.activation(warm2[:], warm[:], SIGMOID)

        rows = x_scales[0].bitcast(I32)
        nc.sync.dma_start(
            out=xs[:].bitcast(I32), in_=rows.unsqueeze(1).to_broadcast([16, 8, T // 4])
        )
        nc.sync.dma_start(offs_t[:], offs)
        nc.sync.dma_start(hc_t[:], hc)
        nc.sync.dma_start(ca_t[:], ca)
        nc.sync.dma_start(
            out=xw[:].bitcast(I32),
            in_=x_words[0].rearrange("p n t -> p (n t)").bitcast(I32),
        )
        w_rows = w1.rearrange("(p j) c -> p j c", j=PACK)
        w_raw = []
        for h in range(2):
            wr = keep.tile([P, PACK, HALF], F32, name="w_raw%d" % h, tag="w_raw%d" % h)
            nc.sync.dma_start(out=wr[:], in_=w_rows[:, :, h * HALF : (h + 1) * HALF])
            w_raw.append(wr)
        nc.sync.dma_start(n1_t[:], n1)
        nc.sync.dma_start(n2_t[:], n2)
        nc.sync.dma_start(n3_t[:], n3)

        def negated_product(dst, slope, threshold, name):
            both = keep.tile([P, PACK], F32, name=name)
            nc.gpsimd.tensor_tensor(both[:], slope[:], threshold[:], MULT)
            nc.gpsimd.tensor_scalar(dst[:], both[:], -1.0, 0.0, MULT, ADD)

        placed_s = keep.tile([P, 3 * S], U8, name="placed_s", align_bytes=64)
        nc.vector.memset(placed_s[:].bitcast(I32), 0)
        picked_s = keep.tile([P, 3 * S], U8, name="picked_s")
        for n, lst in enumerate((offs_t, hc_t, ca_t)):
            nc.vector.tensor_copy(picked_s[:, n * S : (n + 1) * S], xs[:].indirect(lst[:]))
        for a in range(4):
            nc.sync.dma_start(
                out=placed_s[a:P:32, :].bitcast(I32),
                in_=picked_s[8 * a : P : 32, :].bitcast(I32),
            )
        xq_s = placed_s[:, 0:S]
        hc_s = placed_s[:, S : 2 * S]
        ca_s = placed_s[:, 2 * S : 3 * S]
        xq_w = keep.tile([P, S], U32, name="xq_w", align_bytes=64)
        nc.vector.tensor_copy(xq_w[:], xw[:].indirect(offs_t[:]))
        hc_w = keep.tile([P, C], U32, name="hc_w", align_bytes=64)
        nc.vector.tensor_copy(hc_w[:], xw[:].indirect(hc_t[:]))

        wg = keep.tile([P, PACK * P * PACK], BF16, name="wg", align_bytes=64, tag="wg")
        wg_v = wg[:].rearrange("p (t m j) -> p m j t", t=PACK, j=PACK)
        for h in range(2):
            src = w_raw[h][:].rearrange("p j (m t) -> p m j t", t=PACK)
            if h == 0:
                nc.scalar.copy(out=wg_v[:, 0:64], in_=src)
            else:
                nc.scalar.copy(out=wg_v[:, 64 : 64 + SHARE], in_=src[:, 0:SHARE])
                nc.vector.tensor_copy(out=wg_v[:, 64 + SHARE : 128], in_=src[:, SHARE:64])
        sl2_t = keep.tile([P, PACK], F32, name="sl2_t", tag="w_raw0")
        th2_t = keep.tile([P, PACK], F32, name="th2_t", tag="w_raw1")
        with nc.allow_non_contiguous_dma(reason="one value a row"):
            for t_, src in ((sl2_t, sl2), (th2_t, th2)):
                nc.sync.dma_start(out=t_[:], in_=src.rearrange("(c p) o -> p (c o)", p=P))
        wq_w = keep.tile([P, H], U32, name="wq_w", align_bytes=64)
        wq_s = keep.tile([P, H], U8, name="wq_s", align_bytes=64)
        for t in range(PACK):
            nc.vector.quantize_mx(
                out=wq_w[:, t * P : (t + 1) * P].bitcast(FP8X4),
                scales=wq_s[:, t * P : (t + 1) * P],
                in_=wg[:, t * 512 : (t + 1) * 512],
            )

        nb1 = keep.tile([P, PACK], F32, name="nb1")
        negated_product(nb1, sl_t, th_t, "slth")

        y_ps = []
        for t in range(PACK):
            bank = psum.tile([P, S], F32, name="y_ps%d" % t, tag="bank%d" % t)
            nc.tensor.matmul_mx(
                out=bank[:],
                lhsT=wq_w[:, t * P : (t + 1) * P].bitcast(FP8X4),
                lhsT_scale=wq_s[:, t * P : (t + 1) * P],
                rhs=xq_w[:].bitcast(FP8X4),
                rhs_scale=xq_s,
                start=True,
                stop=True,
            )
            y_ps.append(bank)

        ca_w = keep.tile([P, C], U32, name="ca_w", align_bytes=64, tag="wg")
        nc.vector.tensor_copy(ca_w[:], xw[:].indirect(ca_t[:]))

        whole = slice(0, S)
        halves = (slice(0, HALF), slice(HALF, S))

        def offsets(lst, cols):
            return lst[:, cols.start // 16 : cols.stop // 16]

        nc.scalar.copy(row_sb[0][:, 0:S], y_ps[0][:])
        for t in range(1, PACK):
            nc.vector.tensor_copy(row_sb[t][:, 0:S], y_ps[t][:])

        zp = keep.tile([P, PACK, S], BF16, name="zp")
        zq_w = keep.tile([P, S], U32, name="zq_w", align_bytes=64)
        zq_s = keep.tile([P, S], U8, name="zq_s", align_bytes=64)

        def gate(t, cols):
            sg = keep.tile([P, cols.stop - cols.start], F32, name="sg%d_%d" % (t, cols.start), tag="sg%d" % t)
            nc.scalar.activation(
                sg[:],
                row_sb[t][:].indirect(offsets(n1_t, cols)),
                SIGMOID,
                bias=nb1[:, t : t + 1],
                scale=sl_t[:, t : t + 1],
            )
            nc.vector.scalar_tensor_tensor(
                zp[:, t, cols], row_sb[t][:, cols], gs_t[:, t : t + 1], sg[:], MULT, MULT
            )

        def weave(h):
            zi = keep.tile([P, HALF * PACK], BF16, name="zi%d" % h, tag="zi%d" % h, align_bytes=64)
            woven = zi[:].rearrange("p (c i t) -> p c t i", i=4, t=PACK)
            planes = zp[:, :, halves[h]].rearrange("p t (c i) -> p c t i", i=4)
            nc.vector.tensor_copy(woven, planes)
            return zi

        def quantise(h, zi):
            nc.vector.quantize_mx(out=zq_w[:, halves[h]].bitcast(FP8X4), scales=zq_s[:, halves[h]], in_=zi[:])

        def product(bank, words, scales, cols):
            nc.tensor.matmul_mx(
                out=bank[:, cols],
                lhsT=words.bitcast(FP8X4),
                lhsT_scale=scales,
                rhs=zq_w[:, cols].bitcast(FP8X4),
                rhs_scale=zq_s[:, cols],
                start=True,
                stop=True,
            )

        b_ps = {}
        a_ps = {}

        def product_b(c, cols):
            if c not in b_ps:
                b_ps[c] = psum.tile([P, S], F32, name="b_ps%d" % c, tag="bank%d" % (4 + c))
            product(b_ps[c], hc_w[:, c * P : (c + 1) * P], hc_s[:, c * P : (c + 1) * P], cols)

        def product_a(c, cols):
            if c not in a_ps:
                a_ps[c] = psum.tile([P, S], F32, name="a_ps%d" % c, tag="bank%d" % c)
            product(a_ps[c], ca_w[:, c * P : (c + 1) * P], ca_s[:, c * P : (c + 1) * P], cols)

        def leave_b(c, cols):
            nc.scalar.activation(row_sb[c][:, cols], b_ps[c][:, cols], COPY, scale=0.0625)

        def leave_a(c, cols, on_vector):
            if on_vector:
                nc.vector.tensor_scalar(a_sb[c][:, cols], a_ps[c][:, cols], -0.03125, None, MULT)
            else:
                nc.scalar.activation(a_sb[c][:, cols], a_ps[c][:, cols], COPY, scale=-0.03125)

        gate(0, whole)
        for t in range(1, PACK):
            gate(t, halves[0])
        gate(1, halves[1])
        quantise(0, weave(0))
        gate(2, halves[1])
        gate(3, halves[1])
        for c in range(PACK):
            product_b(c, halves[0])
            product_a(c, halves[0])
        quantise(1, weave(1))
        nb2 = keep.tile([P, PACK], F32, name="nb2")
        negated_product(nb2, sl2_t, th2_t, "slth2")
        for c in range(PACK):
            leave_b(c, halves[0])
            leave_a(c, halves[0], False)
        for c in range(PACK):
            product_b(c, halves[1])
            product_a(c, halves[1])
        for c in range(PACK):
            leave_a(c, halves[1], True)

        prod = keep.tile([P, PACK, S], F32, name="prod")
        res = keep.tile([P, PACK, S], F32, name="res")
        last = PACK - 1
        for c in range(PACK):
            leave_b(c, halves[1])
            sg2 = keep.tile([P, S], F32, name="sg2_%d" % c, tag="sg2_%d" % c)
            for cols in halves if c in (0, last) else (whole,):
                nc.scalar.activation(
                    sg2[:, cols],
                    row_sb[c][:].indirect(offsets(n2_t, cols)),
                    SIGMOID,
                    bias=nb2[:, c : c + 1],
                    scale=sl2_t[:, c : c + 1],
                )
            for cols in halves:
                nc.vector.scalar_tensor_tensor(prod[:, c, cols], a_sb[c][:, cols], -2.0, sg2[:, cols], MULT, MULT)
            for h, cols in enumerate(halves):
                picked = a_sb[c][:].indirect(offsets(n3_t, cols))
                if c < last:
                    nc.vector.tensor_tensor(res[:, c, cols], picked, prod[:, c, cols], ADD)
                else:
                    far = keep.tile([P, HALF], F32, name="far%d" % h, tag="sg2_%d" % (1 + h))
                    nc.scalar.activation(far[:], picked, COPY)
                    nc.vector.tensor_tensor(res[:, c, cols], far[:], prod[:, c, cols], ADD)
                    nc.sync.dma_start(out=out[c * P : (c + 1) * P, cols], in_=res[:, c, cols])
            if c < last:
                nc.sync.dma_start(out=out[c * P : (c + 1) * P, :], in_=res[:, c, :])
